import numpy as np
import ml_dtypes

BF16 = ml_dtypes.bfloat16


def bf(x):
    return np.asarray(x, np.float32).astype(BF16)


def f32(x):
    return np.asarray(x, np.float32)


def f64(x):
    return np.asarray(x).astype(np.float64)


def striped(idx):
    return np.concatenate([l.reshape(-1, 16).T for l in idx])


def rows(idx, k):
    return np.tile(np.repeat(idx, 16, axis=0), (k // (16 * 8), 1))


def look(tab, idx):
    return np.take_along_axis(f64(tab), rows(idx, len(tab)), axis=1)


K, S, D, V, N = 128, 2048, 3, 512, 1536


def setup_inputs():
    return {"tab": f32(np.random.standard_normal((K, S))), "u0": f32(np.random.uniform(0.2, 1.0, (K, V))), "u1": f32(np.random.uniform(0.2, 1.0, (K, V))), "u2": f32(np.random.uniform(0.2, 1.0, (K, V))), "offs": striped(np.stack([np.random.permutation(S)[:N] for _ in range(8)]))}


def reference(tab, u0, u1, u2, offs):
    idx = np.stack([g.T.reshape(-1) for g in np.split(offs, 8)])
    x = f64(u0) * np.minimum(np.maximum(look(tab, idx[:, :V]), -1.25), 1.0) + f64(u1) * np.minimum(np.maximum(look(tab, idx[:, 1 * V:2 * V]), -1.25), 1.0) + f64(u2) * np.minimum(np.maximum(look(tab, idx[:, 2 * V:3 * V]), -1.25), 1.0)
    return x

@@ -1,0 +1,45 @@
+import concourse.mybir as mybir
+
+F32, U16 = mybir.dt.float32, mybir.dt.uint16
+ALU = mybir.AluOpType
+
+ROWS = 128
+TABLE = 2048
+V = 512
+D = 3
+LOW, HIGH = -1.25, 1.0
+WORDS = V // 16
+
+
+def tile_lookup_clipmix_out_kernel(tc, tab, u0, u1, u2, offs, out):
+    nc = tc.nc
+    with (
+        tc.tile_pool(name="held", bufs=1) as held,
+        tc.tile_pool(name="work", bufs=1) as work,
+    ):
+        offsets = held.tile([ROWS, D * WORDS], U16, name="offsets")
+        nc.sync.dma_start(offsets[:], offs)
+        table = held.tile([ROWS, TABLE], F32, name="table")
+        nc.scalar.dma_start(table[:], tab)
+
+        weights = []
+        for d, u in enumerate((u0, u1, u2)):
+            w = held.tile([ROWS, V], F32, name=f"weights{d}")
+            nc.scalar.dma_start(w[:], u)
+            weights.append(w)
+
+        products = []
+        for d in range(D):
+            piece = offsets[:, d * WORDS : (d + 1) * WORDS]
+            clamped = work.tile([ROWS, V], F32, name=f"clamped{d}")
+            nc.vector.tensor_scalar(clamped[:], table[:].indirect(piece), LOW, HIGH, ALU.max, ALU.min)
+            product = work.tile([ROWS, V], F32, name=f"product{d}")
+            nc.vector.tensor_tensor(product[:], clamped[:], weights[d][:], ALU.mult)
+            products.append(product)
+
+        total = products[0]
+        for d in range(1, D):
+            wider = work.tile([ROWS, V], F32, name=f"sum{d}")
+            nc.vector.tensor_tensor(wider[:], total[:], products[d][:], ALU.add)
+            total = wider
+        nc.sync.dma_start(out, total[:])

@@ -9,6 +9,7 @@ V = 512
 D = 3
 LOW, HIGH = -1.25, 1.0
 WORDS = V // 16
+HALF = V // 2
 
 
 def tile_lookup_clipmix_out_kernel(tc, tab, u0, u1, u2, offs, out):
@@ -34,12 +35,15 @@ def tile_lookup_clipmix_out_kernel(tc, tab, u0, u1, u2, offs, out):
             clamped = work.tile([ROWS, V], F32, name=f"clamped{d}")
             nc.vector.tensor_scalar(clamped[:], table[:].indirect(piece), LOW, HIGH, ALU.max, ALU.min)
             product = work.tile([ROWS, V], F32, name=f"product{d}")
-            nc.vector.tensor_tensor(product[:], clamped[:], weights[d][:], ALU.mult)
+            engine = nc.vector if d == D - 1 else nc.gpsimd
+            engine.tensor_tensor(product[:], clamped[:], weights[d][:], ALU.mult)
             products.append(product)
 
-        total = products[0]
-        for d in range(1, D):
-            wider = work.tile([ROWS, V], F32, name=f"sum{d}")
-            nc.vector.tensor_tensor(wider[:], total[:], products[d][:], ALU.add)
-            total = wider
-        nc.sync.dma_start(out, total[:])
+        halves = [slice(0, HALF), slice(HALF, V)]
+        partial = [work.tile([ROWS, HALF], F32, name=f"partial{h}") for h in range(2)]
+        total = [work.tile([ROWS, HALF], F32, name=f"total{h}") for h in range(2)]
+        for h, cols in enumerate(halves):
+            nc.vector.tensor_tensor(partial[h][:], products[0][:, cols], products[1][:, cols], ALU.add)
+        for h, cols in enumerate(halves):
+            nc.vector.tensor_tensor(total[h][:], partial[h][:], products[2][:, cols], ALU.add)
+            nc.sync.dma_start(out[:, cols], total[h][:])

import concourse.mybir as mybir

F32, U16 = mybir.dt.float32, mybir.dt.uint16
ALU = mybir.AluOpType

ROWS = 128
TABLE = 2048
V = 512
D = 3
LOW, HIGH = -1.25, 1.0
WORDS = V // 16
HALF = V // 2


def tile_lookup_clipmix_out_kernel(tc, tab, u0, u1, u2, offs, out):
    nc = tc.nc
    with (
        tc.tile_pool(name="held", bufs=1) as held,
        tc.tile_pool(name="work", bufs=1) as work,
    ):
        offsets = held.tile([ROWS, D * WORDS], U16, name="offsets")
        nc.sync.dma_start(offsets[:], offs)
        table = held.tile([ROWS, TABLE], F32, name="table")
        nc.scalar.dma_start(table[:], tab)

        weights = []
        for d, u in enumerate((u0, u1, u2)):
            w = held.tile([ROWS, V], F32, name=f"weights{d}")
            nc.scalar.dma_start(w[:], u)
            weights.append(w)

        products = []
        for d in range(D):
            piece = offsets[:, d * WORDS : (d + 1) * WORDS]
            clamped = work.tile([ROWS, V], F32, name=f"clamped{d}")
            nc.vector.tensor_scalar(clamped[:], table[:].indirect(piece), LOW, HIGH, ALU.max, ALU.min)
            product = work.tile([ROWS, V], F32, name=f"product{d}")
            engine = nc.vector if d == D - 1 else nc.gpsimd
            engine.tensor_tensor(product[:], clamped[:], weights[d][:], ALU.mult)
            products.append(product)

        halves = [slice(0, HALF), slice(HALF, V)]
        partial = [work.tile([ROWS, HALF], F32, name=f"partial{h}") for h in range(2)]
        total = [work.tile([ROWS, HALF], F32, name=f"total{h}") for h in range(2)]
        for h, cols in enumerate(halves):
            nc.vector.tensor_tensor(partial[h][:], products[0][:, cols], products[1][:, cols], ALU.add)
        for h, cols in enumerate(halves):
            nc.vector.tensor_tensor(total[h][:], partial[h][:], products[2][:, cols], ALU.add)
            nc.sync.dma_start(out[:, cols], total[h][:])
